import numpy as np
import ml_dtypes


def mxq(x, axis, fmt="e4m3"):
    dtype, down = {"e4m3": (ml_dtypes.float8_e4m3fn, 7), "e5m2": (ml_dtypes.float8_e5m2, 14)}[fmt]
    v = np.moveaxis(np.asarray(x, np.float32).astype(ml_dtypes.bfloat16).astype(np.float64), axis, -1)
    blocks = v.reshape(v.shape[:-1] + (-1, 32))
    amax = np.abs(blocks).max(-1, keepdims=True)
    byte = np.maximum(np.where(amax > 0, np.frexp(amax)[1] - 1 + 127, 0) - down, 1)
    scale = np.exp2(byte - 127.0)
    codes = (blocks / scale).astype(np.float32).astype(dtype).astype(np.float64)
    return np.moveaxis((codes * scale).reshape(v.shape), -1, axis)


WIDE = False


def mx_kscale(k):
    if not WIDE:
        return np.ones(k)
    levels = np.array([10, -10, 5, -5, 0])
    if k % 512:
        return np.exp2(np.random.permutation(np.resize(levels, k // 32))).repeat(32)
    a = np.empty((k // 512, 16))
    for p in range(k // 512):
        a[p, :8] = np.random.permutation(np.resize(levels, 8))
        for g in range(8):
            far = levels[np.abs(levels - a[p, g]) >= 10]
            a[p, g + 8] = far[np.random.randint(len(far))]
    return np.exp2(a.ravel()).repeat(32)


def f64(x):
    return np.asarray(x).astype(np.float64)


def striped(idx):
    return np.tile(np.asarray(idx).reshape(-1, 16).T, (8, 1)).astype(np.uint16)


def unstriped(offs):
    return offs[:16].T.reshape(-1).astype(np.int64)


E2M1 = np.array([0.0, 0.5, 1.0, 1.5, 2.0, 3.0, 4.0, 6.0, -0.0, -0.5, -1.0, -1.5, -2.0, -3.0, -4.0, -6.0])


def pack_weight(w, fmt):
    k, n = w.shape
    w = f64(np.asarray(w, np.float32).astype(ml_dtypes.bfloat16)).reshape(k // 32, 32, n)
    amax = np.abs(w).max(1)
    if fmt == "e4m3":
        byte = np.frexp(amax)[1] - 1 + 127 - 7
    else:
        mant, ex = np.frexp(amax / 6.0)
        byte = np.where(mant > 0.5, ex, ex - 1) + 127
    byte = np.clip(np.where(amax > 0, byte, 1), 1, 254)
    scaled = (w * np.exp2(127.0 - byte)[:, None, :]).reshape(k, n).astype(np.float32)
    by_word = np.ascontiguousarray(scaled.reshape(k // 512, 128, 4, n).transpose(0, 1, 3, 2))
    if fmt == "e4m3":
        words = by_word.astype(ml_dtypes.float8_e4m3fn).view(np.uint8)
    else:
        c = by_word.astype(ml_dtypes.float4_e2m1fn).view(np.uint8) & 0xF
        words = (c[..., 0::2] | (c[..., 1::2] << 4)).reshape(k // 512, 128, 2 * n)
    return np.ascontiguousarray(words), np.ascontiguousarray(byte.astype(np.uint8).reshape(k // 512, 16, n))


def unpack_weight(words, scales, fmt):
    g, _, n = scales.shape
    words = np.ascontiguousarray(words).reshape(g, 128, n, -1)
    if fmt == "e4m3":
        vals = words.view(ml_dtypes.float8_e4m3fn).astype(np.float64)
    else:
        nib = np.empty((g, 128, n, 4), np.uint8)
        nib[..., 0::2] = words & 0xF
        nib[..., 1::2] = words >> 4
        vals = E2M1[nib]
    vals = vals * np.repeat(np.exp2(scales.astype(np.float64) - 127.0), 8, axis=1)[..., None]
    return vals.transpose(0, 1, 3, 2).reshape(g * 512, n)


def bf(x):
    return np.asarray(x, np.float32).astype(ml_dtypes.bfloat16)


def planes(Y):
    r, m = Y.shape
    b = f64(bf(Y)).reshape(r // 32, 32, m)
    amax = np.abs(b).max(1)
    byte = np.clip(np.where(amax > 0, np.frexp(amax)[1] - 1 + 127 - 7, 1), 1, 254)
    codes = (b * np.exp2(127.0 - byte)[:, None, :]).reshape(r, m).astype(np.float32).astype(ml_dtypes.float8_e4m3fn).view(np.uint8)
    words = codes.reshape(r // 512, 128, 4, m).transpose(0, 1, 3, 2)
    return np.ascontiguousarray(words), np.ascontiguousarray(byte.astype(np.uint8).reshape(r // 512, 16, m))


K, D, T, I, Q = 512, 512, 1024, 256, 512


def setup_inputs():
    n = np.random.standard_normal
    idx = np.random.permutation(T)[:I]
    fk = mx_kscale(K)
    fd = mx_kscale(D)
    hidp = pack_weight(n((K, T)) / fk[:, None], "e2m1")
    return {
        "wk": (n((K, D)) * 1 / np.sqrt(K) * fk[:, None] / fd).astype(np.float32),
        "hid_words": hidp[0],
        "hid_scales": hidp[1],
        "keys": (n((D, T)) / fd[:, None]).astype(np.float32),
        "trust": (np.random.uniform(0.5, 1.0, (1, I))).astype(np.float32),
        "query": (n((D, Q)) * 0.7 / np.sqrt(D) * fd[:, None]).astype(np.float32),
        "offs": striped(idx),
    }


def reference(wk, hid_words, hid_scales, keys, trust, query, offs):
    idx = unstriped(offs)
    hidu = unpack_weight(hid_words, hid_scales, "e2m1")
    wkq = mxq(f64(wk), 0, "e4m3")
    hididxg = hidu[:, idx]
    kn = wkq.T @ hididxg
    dl = (kn - f64(keys)[:, idx]) * f64(trust)
    df = np.zeros((D, T))
    df[:, idx] = dl
    km = df + f64(keys)
    queryq = mxq(f64(query), 0, "e4m3")
    kmq = mxq(km, 0, "e4m3")
    a = queryq.T @ kmq
    p = np.exp(a - np.max(a, axis=1, keepdims=True))
    y = p / np.sum(p, axis=1, keepdims=True) * 512.0
    words, scales = planes(y)
    return y, words, scales

@@ -1,0 +1,277 @@
+from contextlib import ExitStack
+
+import concourse.mybir as mybir
+
+K, D, T, I, Q = 512, 512, 1024, 256, 512
+FLOPS = 2 * K * D * I + 2 * D * Q * T
+
+F32 = mybir.dt.float32
+BF16 = mybir.dt.bfloat16
+I32 = mybir.dt.int32
+U32 = mybir.dt.uint32
+U16 = mybir.dt.uint16
+U8 = mybir.dt.uint8
+FP8X4 = mybir.dt.float8_e4m3fn_x4
+FP4X4 = mybir.dt.float4_e2m1fn_x4
+ALU = mybir.AluOpType
+ACT = mybir.ActivationFunctionType
+AXIS = mybir.AxisListType
+
+P = 128
+PACK = 4
+BANK = 512
+HALVES = T // BANK
+
+
+def deal(copy, dealt, raw, half, pair):
+    m = slice(half * 64, (half + 1) * 64)
+    copy(
+        dealt[:].rearrange("p (t m j) -> p m j t", t=2, j=PACK)[:, m],
+        raw[:].rearrange("p j (m t) -> p m j t", t=PACK)[:, :, :, 2 * pair : 2 * pair + 2],
+    )
+
+
+def weave(copy, woven, planes):
+    copy(
+        woven[:].rearrange("p (c i t) -> p c t i", i=4, t=PACK),
+        planes.rearrange("p t (c i) -> p c t i", i=4),
+    )
+
+
+def quantize(nc, codes, scales, cols, woven):
+    nc.vector.quantize_mx(out=codes[:, cols].bitcast(FP8X4), scales=scales[:, cols], in_=woven[:])
+
+
+def tile_attend_blendrepair_pl_kernel(tc, wk, hid_words, hid_scales, keys, trust, query, offs, out_0, out_1, out_2):
+    nc = tc.nc
+    with ExitStack() as ctx:
+        sb = ctx.enter_context(tc.tile_pool(name="sb", bufs=1))
+        ps = ctx.enter_context(tc.psum_pool(name="ps", bufs=1))
+
+        def scalar_cast(out, in_):
+            nc.scalar.activation(out, in_, ACT.Copy)
+
+        offsets = sb.tile([P, I // 16], U16, name="offsets")
+        nc.sync.dma_start(offsets[:], offs)
+
+        hid_s = sb.tile([P, T], U8, name="hid_s", align_bytes=64)
+        nc.vector.memset(hid_s[:].bitcast(I32), 0)
+        for quad in range(4):
+            nc.scalar.dma_start(
+                hid_s[32 * quad : 32 * quad + 4, :].bitcast(I32), hid_scales[0, 4 * quad : 4 * quad + 4, :].bitcast(I32)
+            )
+
+        hid_w = sb.tile([P, T], U16, name="hid_w", align_bytes=64)
+        nc.sync.dma_start(hid_w[:].bitcast(I32), hid_words[0].bitcast(I32))
+        wk_rows = wk.rearrange("(p j) c -> p j c", j=PACK)
+        wk_raw = []
+        for half in range(2):
+            raw = sb.tile([P, PACK, D // 2], F32, name=f"wk_raw{half}")
+            nc.sync.dma_start(raw[:], wk_rows[:, :, half * 256 : (half + 1) * 256])
+            wk_raw.append(raw)
+        trust_all = sb.tile([P, I], F32, name="trust_all")
+        nc.sync.dma_start(trust_all[:], trust[0].partition_broadcast(P))
+        key_rows = keys.rearrange("(p t) c -> p t c", t=PACK)
+        key_planes = []
+        for t in range(PACK):
+            plane = sb.tile([P, T], F32, name=f"keys{t}")
+            nc.sync.dma_start(plane[:], key_rows[:, t, :])
+            key_planes.append(plane)
+        q_rows = query.rearrange("(p j) c -> p j c", j=PACK)
+        q_raw = []
+        for half in range(2):
+            raw = sb.tile([P, PACK, Q // 2], F32, name=f"q_raw{half}")
+            nc.sync.dma_start(raw[:], q_rows[:, :, half * 256 : (half + 1) * 256])
+            q_raw.append(raw)
+
+        df = []
+        for t in range(PACK):
+            window = sb.tile([P, T], F32, name=f"df{t}")
+            (nc.vector if t < 2 else nc.gpsimd).memset(window[:], 0.0)
+            df.append(window)
+
+        got_w = sb.tile([P, I], U16, name="got_w", align_bytes=64)
+        got_s = sb.tile([P, I], U8, name="got_s", align_bytes=64)
+        nc.vector.tensor_copy(got_w[:], hid_w[:].indirect(offsets[:]))
+        nc.vector.tensor_copy(got_s[:], hid_s[:].indirect(offsets[:]))
+        wk_bf = [sb.tile([P, D * 2], BF16, name=f"wk_bf{pair}", align_bytes=64) for pair in range(2)]
+        wk_codes = sb.tile([P, D], U32, name="wk_codes", align_bytes=64)
+        wk_scales = sb.tile([P, D], U8, name="wk_scales", align_bytes=64)
+        for half in range(2):
+            deal(nc.vector.tensor_copy, wk_bf[0], wk_raw[half], half, 0)
+            deal(scalar_cast, wk_bf[1], wk_raw[half], half, 1)
+        for pair in range(2):
+            quantize(nc, wk_codes, wk_scales, slice(pair * 256, (pair + 1) * 256), wk_bf[pair])
+
+        kn, old, diff, dl = [], [], [], []
+        for t in range(PACK):
+            cols = slice(t * P, (t + 1) * P)
+            fresh = ps.tile([P, I], F32, name=f"kn{t}", tag=f"bank{4 + t}")
+            nc.tensor.matmul_mx(
+                out=fresh[:],
+                lhsT=wk_codes[:, cols].bitcast(FP8X4),
+                lhsT_scale=wk_scales[:, cols],
+                rhs=got_w[:].bitcast(U8).bitcast(FP4X4),
+                rhs_scale=got_s[:],
+                start=True,
+                stop=True,
+            )
+            kn.append(fresh)
+            dl.append(sb.tile([P, I], F32, name=f"dl{t}", tag=f"weighed{t}", align_bytes=64))
+
+        def gather(t):
+            old.append(sb.tile([P, I], F32, name=f"old{t}", tag="shared0" if t >= 2 else f"old{t}", align_bytes=64))
+            listed = key_planes[t][:].indirect(offsets[:])
+            if t == 1:
+                nc.scalar.activation(old[t][:], listed, ACT.Copy)
+            else:
+                nc.vector.tensor_copy(old[t][:], listed)
+
+        def subtract(t):
+            diff.append(sb.tile([P, I], F32, name=f"diff{t}", tag=f"shared{t}", align_bytes=64))
+            nc.vector.tensor_tensor(diff[t][:], kn[t][:], old[t][:], ALU.subtract)
+
+        def weigh(t):
+            nc.vector.tensor_tensor(dl[t][:], diff[t][:], trust_all[:], ALU.mult)
+
+        def scatter(t):
+            nc.scalar.activation(df[t][:].indirect(offsets[:]), dl[t][:], ACT.Copy)
+
+        gather(0)
+        gather(1)
+        subtract(0)
+        weigh(0)
+        subtract(1)
+        gather(2)
+        weigh(1)
+        subtract(2)
+        gather(3)
+        weigh(2)
+        subtract(3)
+        weigh(3)
+        for t in range(PACK):
+            scatter(t)
+
+        km_planes = [
+            sb.tile([P, PACK, BANK], BF16, name=f"km_planes{h}", tag=f"shared{3 - h}", align_bytes=64) for h in range(HALVES)
+        ]
+        q_bf = [
+            sb.tile([P, Q * 2], BF16, name="q_bf0", align_bytes=64),
+            sb.tile([P, Q * 2], BF16, name="q_bf1", tag="weighed3", align_bytes=64),
+        ]
+        q_codes = sb.tile([P, Q], U32, name="q_codes", align_bytes=64)
+        q_scales = sb.tile([P, Q], U8, name="q_scales", align_bytes=64)
+
+        def repair(t):
+            for h in range(HALVES):
+                cols = slice(h * BANK, (h + 1) * BANK)
+                nc.vector.tensor_tensor(km_planes[h][:, t, :], df[t][:, cols], key_planes[t][:, cols], ALU.add)
+
+        for t in range(PACK - 1):
+            repair(t)
+        for half in range(2):
+            deal(nc.vector.tensor_copy, q_bf[0], q_raw[half], half, 0)
+            deal(nc.scalar.copy, q_bf[1], q_raw[half], half, 1)
+        quantize(nc, q_codes, q_scales, slice(0, 256), q_bf[0])
+        repair(PACK - 1)
+
+        km_codes = sb.tile([P, T], U32, name="km_codes", align_bytes=64)
+        km_scales = sb.tile([P, T], U8, name="km_scales", align_bytes=64)
+        km_bf = [sb.tile([P, BANK * PACK], BF16, name=f"km_bf{h}", align_bytes=64) for h in range(HALVES)]
+        weave(nc.vector.tensor_copy, km_bf[0], km_planes[0][:])
+        weave(nc.scalar.copy, km_bf[1], km_planes[1][:])
+        quantize(nc, km_codes, km_scales, slice(0, BANK), km_bf[0])
+        quantize(nc, q_codes, q_scales, slice(256, 512), q_bf[1])
+
+        neg_half = sb.tile([P, PACK, HALVES], F32, name="neg_half")
+        neg_max = sb.tile([P, PACK], F32, name="neg_max")
+        sum_half = sb.tile([P, PACK, HALVES], F32, name="sum_half")
+        rescale = sb.tile([P, PACK, HALVES], F32, name="rescale")
+        share = sb.tile([P, PACK, HALVES], F32, name="share")
+        total = sb.tile([P, PACK], F32, name="total")
+        inverse = sb.tile([P, PACK], F32, name="inverse")
+        y = sb.tile([P, PACK, T], F32, name="y")
+        y_rows = out_0.rearrange("(p r) c -> p r c", r=PACK)
+        weights = [sb.tile([P, T], F32, name=f"p{r}") for r in range(PACK)]
+
+        def score(r, h):
+            rows = slice(r * P, (r + 1) * P)
+            cols = slice(h * BANK, (h + 1) * BANK)
+            bank = ps.tile([P, BANK], F32, name=f"a{r}{h}", tag=f"bank{2 * r + h}")
+            nc.tensor.matmul_mx(
+                out=bank[:],
+                lhsT=q_codes[:, rows].bitcast(FP8X4),
+                lhsT_scale=q_scales[:, rows],
+                rhs=km_codes[:, cols].bitcast(FP8X4),
+                rhs_scale=km_scales[:, cols],
+                start=True,
+                stop=True,
+            )
+            nc.vector.tensor_reduce(neg_half[:, r, h : h + 1], bank[:], AXIS.X, ALU.max, negate=True)
+            nc.scalar.activation(
+                weights[r][:, cols], bank[:], ACT.Exp, bias=neg_half[:, r, h : h + 1], accum_out=sum_half[:, r, h : h + 1]
+            )
+
+        def join(r):
+            one = slice(r, r + 1)
+            nc.vector.tensor_tensor(neg_max[:, one], neg_half[:, r, 0:1], neg_half[:, r, 1:2], ALU.min)
+            nc.scalar.activation(rescale[:, r, :], neg_half[:, r, :], ACT.Exp, bias=neg_max[:, one], scale=-1.0)
+
+        def invert(r):
+            one = slice(r, r + 1)
+            nc.vector.scalar_tensor_tensor(
+                share[:, r, :], sum_half[:, r, :], 1.0 / 512.0, rescale[:, r, :], ALU.mult, ALU.mult, accum_out=total[:, one]
+            )
+            nc.vector.reciprocal(inverse[:, one], total[:, one])
+
+        def normalise(r, h):
+            cols = slice(h * BANK, (h + 1) * BANK)
+            nc.vector.tensor_scalar(
+                y[:, r, cols], weights[r][:, cols], rescale[:, r, h : h + 1], inverse[:, r : r + 1], ALU.mult, ALU.mult
+            )
+
+        def finish(r):
+            normalise(r, 0)
+            normalise(r, 1)
+            nc.sync.dma_start(y_rows[:, r, :], y[:, r, :])
+
+        score(0, 0)
+        quantize(nc, km_codes, km_scales, slice(BANK, T), km_bf[1])
+        score(1, 0)
+        score(0, 1)
+        join(0)
+        score(1, 1)
+        join(1)
+        score(2, 0)
+        invert(0)
+        score(2, 1)
+        join(2)
+        finish(0)
+        invert(1)
+        score(3, 0)
+        score(3, 1)
+        join(3)
+        finish(1)
+        invert(2)
+        finish(2)
+        invert(3)
+        normalise(3, 1)
+        normalise(3, 0)
+        nc.sync.dma_start(y_rows[:, 3, :], y[:, 3, :])
+
+        y_codes = sb.tile([P, T], U32, name="y_codes", align_bytes=64)
+        y_scales = sb.tile([P, T], U8, name="y_scales", align_bytes=64)
+        word_rows = out_1[0].rearrange("p c t -> p (c t)").bitcast(I32)
+        units = (slice(0, 256), slice(256, 640), slice(640, T))
+        y_bf = [sb.tile([P, (c.stop - c.start) * PACK], BF16, name=f"y_bf{u}", align_bytes=64) for u, c in enumerate(units)]
+        weave(nc.scalar.copy, y_bf[2], y[:, :, units[2]])
+        weave(nc.vector.tensor_copy, y_bf[0], y[:, :, units[0]])
+        weave(nc.vector.tensor_copy, y_bf[1], y[:, :, units[1]])
+        for u, cols in enumerate(units):
+            quantize(nc, y_codes, y_scales, cols, y_bf[u])
+            nc.sync.dma_start(word_rows[:, cols], y_codes[:, cols].bitcast(I32))
+        for quad in range(4):
+            queue = nc.scalar if quad % 2 else nc.sync
+            queue.dma_start(
+                out_2[0, 4 * quad : 4 * quad + 4, :].bitcast(I32), y_scales[32 * quad : 32 * quad + 4, :].bitcast(I32)
+            )

@@ -1,6 +1,7 @@
 from contextlib import ExitStack
 
 import concourse.mybir as mybir
+from concourse.masks import make_identity
 
 K, D, T, I, Q = 512, 512, 1024, 256, 512
 FLOPS = 2 * K * D * I + 2 * D * Q * T
@@ -23,11 +24,11 @@ BANK = 512
 HALVES = T // BANK
 
 
-def deal(copy, dealt, raw, half, pair):
+def deal(copy, dealt, raw, half, planes):
     m = slice(half * 64, (half + 1) * 64)
     copy(
-        dealt[:].rearrange("p (t m j) -> p m j t", t=2, j=PACK)[:, m],
-        raw[:].rearrange("p j (m t) -> p m j t", t=PACK)[:, :, :, 2 * pair : 2 * pair + 2],
+        dealt[:].rearrange("p (t m j) -> p m j t", m=P, j=PACK)[:, m],
+        raw[:].rearrange("p j (m t) -> p m j t", t=PACK)[:, :, :, planes],
     )
 
 
@@ -54,6 +55,17 @@ def tile_attend_blendrepair_pl_kernel(tc, wk, hid_words, hid_scales, keys, trust
         offsets = sb.tile([P, I // 16], U16, name="offsets")
         nc.sync.dma_start(offsets[:], offs)
 
+        trust_col = sb.tile([P, 2], F32, name="trust_col")
+        nc.sync.dma_start(trust_col[:], trust.rearrange("o (p e) -> p (o e)", e=2))
+        identity = sb.tile([P, P], F32, name="identity")
+        make_identity(nc, identity[:])
+        first_bank = ps.tile([P, 2, I], F32, name="first_bank", tag="bank4")
+        trust_all = first_bank[:, 1, :].rearrange("p (e n) -> p e n", e=2)
+        trust_wide = sb.tile([P, 2, P], F32, name="trust_wide")
+        scalar_cast(trust_wide[:], trust_col[:].unsqueeze(2).to_broadcast([P, 2, P]))
+        for e in range(2):
+            nc.tensor.transpose(trust_all[:, e, :], trust_wide[:, e, :], identity[:])
+
         hid_s = sb.tile([P, T], U8, name="hid_s", align_bytes=64)
         nc.vector.memset(hid_s[:].bitcast(I32), 0)
         for quad in range(4):
@@ -69,8 +81,6 @@ def tile_attend_blendrepair_pl_kernel(tc, wk, hid_words, hid_scales, keys, trust
             raw = sb.tile([P, PACK, D // 2], F32, name=f"wk_raw{half}")
             nc.sync.dma_start(raw[:], wk_rows[:, :, half * 256 : (half + 1) * 256])
             wk_raw.append(raw)
-        trust_all = sb.tile([P, I], F32, name="trust_all")
-        nc.sync.dma_start(trust_all[:], trust[0].partition_broadcast(P))
         key_rows = keys.rearrange("(p t) c -> p t c", t=PACK)
         key_planes = []
         for t in range(PACK):
@@ -87,7 +97,7 @@ def tile_attend_blendrepair_pl_kernel(tc, wk, hid_words, hid_scales, keys, trust
         df = []
         for t in range(PACK):
             window = sb.tile([P, T], F32, name=f"df{t}")
-            (nc.vector if t < 2 else nc.gpsimd).memset(window[:], 0.0)
+            (nc.vector if t < 3 else nc.gpsimd).memset(window[:], 0.0)
             df.append(window)
 
         got_w = sb.tile([P, I], U16, name="got_w", align_bytes=64)
@@ -98,17 +108,17 @@ def tile_attend_blendrepair_pl_kernel(tc, wk, hid_words, hid_scales, keys, trust
         wk_codes = sb.tile([P, D], U32, name="wk_codes", align_bytes=64)
         wk_scales = sb.tile([P, D], U8, name="wk_scales", align_bytes=64)
         for half in range(2):
-            deal(nc.vector.tensor_copy, wk_bf[0], wk_raw[half], half, 0)
-            deal(scalar_cast, wk_bf[1], wk_raw[half], half, 1)
+            deal(nc.vector.tensor_copy, wk_bf[0], wk_raw[half], half, slice(0, 2))
+            deal(scalar_cast, wk_bf[1], wk_raw[half], half, slice(2, 4))
         for pair in range(2):
             quantize(nc, wk_codes, wk_scales, slice(pair * 256, (pair + 1) * 256), wk_bf[pair])
 
         kn, old, diff, dl = [], [], [], []
         for t in range(PACK):
             cols = slice(t * P, (t + 1) * P)
-            fresh = ps.tile([P, I], F32, name=f"kn{t}", tag=f"bank{4 + t}")
+            fresh = first_bank[:, 0, :] if t == 0 else ps.tile([P, I], F32, name=f"kn{t}", tag=f"bank{4 + t}")[:]
             nc.tensor.matmul_mx(
-                out=fresh[:],
+                out=fresh,
                 lhsT=wk_codes[:, cols].bitcast(FP8X4),
                 lhsT_scale=wk_scales[:, cols],
                 rhs=got_w[:].bitcast(U8).bitcast(FP4X4),
@@ -120,7 +130,7 @@ def tile_attend_blendrepair_pl_kernel(tc, wk, hid_words, hid_scales, keys, trust
             dl.append(sb.tile([P, I], F32, name=f"dl{t}", tag=f"weighed{t}", align_bytes=64))
 
         def gather(t):
-            old.append(sb.tile([P, I], F32, name=f"old{t}", tag="shared0" if t >= 2 else f"old{t}", align_bytes=64))
+            old.append(sb.tile([P, I], F32, name=f"old{t}", tag="old" if t >= 1 else "old0", align_bytes=64))
             listed = key_planes[t][:].indirect(offsets[:])
             if t == 1:
                 nc.scalar.activation(old[t][:], listed, ACT.Copy)
@@ -128,11 +138,16 @@ def tile_attend_blendrepair_pl_kernel(tc, wk, hid_words, hid_scales, keys, trust
                 nc.vector.tensor_copy(old[t][:], listed)
 
         def subtract(t):
-            diff.append(sb.tile([P, I], F32, name=f"diff{t}", tag=f"shared{t}", align_bytes=64))
-            nc.vector.tensor_tensor(diff[t][:], kn[t][:], old[t][:], ALU.subtract)
+            diff.append(sb.tile([P, I], F32, name=f"diff{t}", tag="diff" if t < 3 else "diff3", align_bytes=64))
+            nc.vector.tensor_tensor(diff[t][:], kn[t], old[t][:], ALU.subtract)
 
         def weigh(t):
-            nc.vector.tensor_tensor(dl[t][:], diff[t][:], trust_all[:], ALU.mult)
+            nc.vector.tensor_tensor(
+                dl[t][:].rearrange("p (n e) -> p n e", e=2),
+                diff[t][:].rearrange("p (n e) -> p n e", e=2),
+                trust_all.rearrange("p e n -> p n e"),
+                ALU.mult,
+            )
 
         def scatter(t):
             nc.scalar.activation(df[t][:].indirect(offsets[:]), dl[t][:], ACT.Copy)
@@ -142,23 +157,20 @@ def tile_attend_blendrepair_pl_kernel(tc, wk, hid_words, hid_scales, keys, trust
         subtract(0)
         weigh(0)
         subtract(1)
-        gather(2)
         weigh(1)
+        gather(2)
         subtract(2)
-        gather(3)
         weigh(2)
+        gather(3)
         subtract(3)
         weigh(3)
         for t in range(PACK):
             scatter(t)
 
         km_planes = [
-            sb.tile([P, PACK, BANK], BF16, name=f"km_planes{h}", tag=f"shared{3 - h}", align_bytes=64) for h in range(HALVES)
+            sb.tile([P, PACK, BANK], BF16, name=f"km_planes{h}", tag=("diff", "old")[h], align_bytes=64) for h in range(HALVES)
         ]
-        q_bf = [
-            sb.tile([P, Q * 2], BF16, name="q_bf0", align_bytes=64),
-            sb.tile([P, Q * 2], BF16, name="q_bf1", tag="weighed3", align_bytes=64),
-        ]
+        q_bf = sb.tile([P, Q * PACK], BF16, name="q_bf", tag="weighed3", align_bytes=64)
         q_codes = sb.tile([P, Q], U32, name="q_codes", align_bytes=64)
         q_scales = sb.tile([P, Q], U8, name="q_scales", align_bytes=64)
 
@@ -170,9 +182,7 @@ def tile_attend_blendrepair_pl_kernel(tc, wk, hid_words, hid_scales, keys, trust
         for t in range(PACK - 1):
             repair(t)
         for half in range(2):
-            deal(nc.vector.tensor_copy, q_bf[0], q_raw[half], half, 0)
-            deal(nc.scalar.copy, q_bf[1], q_raw[half], half, 1)
-        quantize(nc, q_codes, q_scales, slice(0, 256), q_bf[0])
+            deal(nc.scalar.copy, q_bf, q_raw[half], half, slice(0, PACK))
         repair(PACK - 1)
 
         km_codes = sb.tile([P, T], U32, name="km_codes", align_bytes=64)
@@ -180,8 +190,8 @@ def tile_attend_blendrepair_pl_kernel(tc, wk, hid_words, hid_scales, keys, trust
         km_bf = [sb.tile([P, BANK * PACK], BF16, name=f"km_bf{h}", align_bytes=64) for h in range(HALVES)]
         weave(nc.vector.tensor_copy, km_bf[0], km_planes[0][:])
         weave(nc.scalar.copy, km_bf[1], km_planes[1][:])
+        quantize(nc, q_codes, q_scales, slice(0, Q), q_bf)
         quantize(nc, km_codes, km_scales, slice(0, BANK), km_bf[0])
-        quantize(nc, q_codes, q_scales, slice(256, 512), q_bf[1])
 
         neg_half = sb.tile([P, PACK, HALVES], F32, name="neg_half")
         neg_max = sb.tile([P, PACK], F32, name="neg_max")

from contextlib import ExitStack

import concourse.mybir as mybir
from concourse.masks import make_identity

K, D, T, I, Q = 512, 512, 1024, 256, 512
FLOPS = 2 * K * D * I + 2 * D * Q * T

F32 = mybir.dt.float32
BF16 = mybir.dt.bfloat16
I32 = mybir.dt.int32
U32 = mybir.dt.uint32
U16 = mybir.dt.uint16
U8 = mybir.dt.uint8
FP8X4 = mybir.dt.float8_e4m3fn_x4
FP4X4 = mybir.dt.float4_e2m1fn_x4
ALU = mybir.AluOpType
ACT = mybir.ActivationFunctionType
AXIS = mybir.AxisListType

P = 128
PACK = 4
BANK = 512
HALVES = T // BANK


def deal(copy, dealt, raw, half, planes):
    m = slice(half * 64, (half + 1) * 64)
    copy(
        dealt[:].rearrange("p (t m j) -> p m j t", m=P, j=PACK)[:, m],
        raw[:].rearrange("p j (m t) -> p m j t", t=PACK)[:, :, :, planes],
    )


def weave(copy, woven, planes):
    copy(
        woven[:].rearrange("p (c i t) -> p c t i", i=4, t=PACK),
        planes.rearrange("p t (c i) -> p c t i", i=4),
    )


def quantize(nc, codes, scales, cols, woven):
    nc.vector.quantize_mx(out=codes[:, cols].bitcast(FP8X4), scales=scales[:, cols], in_=woven[:])


def tile_attend_blendrepair_pl_kernel(tc, wk, hid_words, hid_scales, keys, trust, query, offs, out_0, out_1, out_2):
    nc = tc.nc
    with ExitStack() as ctx:
        sb = ctx.enter_context(tc.tile_pool(name="sb", bufs=1))
        ps = ctx.enter_context(tc.psum_pool(name="ps", bufs=1))

        def scalar_cast(out, in_):
            nc.scalar.activation(out, in_, ACT.Copy)

        offsets = sb.tile([P, I // 16], U16, name="offsets")
        nc.sync.dma_start(offsets[:], offs)

        trust_col = sb.tile([P, 2], F32, name="trust_col")
        nc.sync.dma_start(trust_col[:], trust.rearrange("o (p e) -> p (o e)", e=2))
        identity = sb.tile([P, P], F32, name="identity")
        make_identity(nc, identity[:])
        first_bank = ps.tile([P, 2, I], F32, name="first_bank", tag="bank4")
        trust_all = first_bank[:, 1, :].rearrange("p (e n) -> p e n", e=2)
        trust_wide = sb.tile([P, 2, P], F32, name="trust_wide")
        scalar_cast(trust_wide[:], trust_col[:].unsqueeze(2).to_broadcast([P, 2, P]))
        for e in range(2):
            nc.tensor.transpose(trust_all[:, e, :], trust_wide[:, e, :], identity[:])

        hid_s = sb.tile([P, T], U8, name="hid_s", align_bytes=64)
        nc.vector.memset(hid_s[:].bitcast(I32), 0)
        for quad in range(4):
            nc.scalar.dma_start(
                hid_s[32 * quad : 32 * quad + 4, :].bitcast(I32), hid_scales[0, 4 * quad : 4 * quad + 4, :].bitcast(I32)
            )

        hid_w = sb.tile([P, T], U16, name="hid_w", align_bytes=64)
        nc.sync.dma_start(hid_w[:].bitcast(I32), hid_words[0].bitcast(I32))
        wk_rows = wk.rearrange("(p j) c -> p j c", j=PACK)
        wk_raw = []
        for half in range(2):
            raw = sb.tile([P, PACK, D // 2], F32, name=f"wk_raw{half}")
            nc.sync.dma_start(raw[:], wk_rows[:, :, half * 256 : (half + 1) * 256])
            wk_raw.append(raw)
        key_rows = keys.rearrange("(p t) c -> p t c", t=PACK)
        key_planes = []
        for t in range(PACK):
            plane = sb.tile([P, T], F32, name=f"keys{t}")
            nc.sync.dma_start(plane[:], key_rows[:, t, :])
            key_planes.append(plane)
        q_rows = query.rearrange("(p j) c -> p j c", j=PACK)
        q_raw = []
        for half in range(2):
            raw = sb.tile([P, PACK, Q // 2], F32, name=f"q_raw{half}")
            nc.sync.dma_start(raw[:], q_rows[:, :, half * 256 : (half + 1) * 256])
            q_raw.append(raw)

        df = []
        for t in range(PACK):
            window = sb.tile([P, T], F32, name=f"df{t}")
            (nc.vector if t < 3 else nc.gpsimd).memset(window[:], 0.0)
            df.append(window)

        got_w = sb.tile([P, I], U16, name="got_w", align_bytes=64)
        got_s = sb.tile([P, I], U8, name="got_s", align_bytes=64)
        nc.vector.tensor_copy(got_w[:], hid_w[:].indirect(offsets[:]))
        nc.vector.tensor_copy(got_s[:], hid_s[:].indirect(offsets[:]))
        wk_bf = [sb.tile([P, D * 2], BF16, name=f"wk_bf{pair}", align_bytes=64) for pair in range(2)]
        wk_codes = sb.tile([P, D], U32, name="wk_codes", align_bytes=64)
        wk_scales = sb.tile([P, D], U8, name="wk_scales", align_bytes=64)
        for half in range(2):
            deal(nc.vector.tensor_copy, wk_bf[0], wk_raw[half], half, slice(0, 2))
            deal(scalar_cast, wk_bf[1], wk_raw[half], half, slice(2, 4))
        for pair in range(2):
            quantize(nc, wk_codes, wk_scales, slice(pair * 256, (pair + 1) * 256), wk_bf[pair])

        kn, old, diff, dl = [], [], [], []
        for t in range(PACK):
            cols = slice(t * P, (t + 1) * P)
            fresh = first_bank[:, 0, :] if t == 0 else ps.tile([P, I], F32, name=f"kn{t}", tag=f"bank{4 + t}")[:]
            nc.tensor.matmul_mx(
                out=fresh,
                lhsT=wk_codes[:, cols].bitcast(FP8X4),
                lhsT_scale=wk_scales[:, cols],
                rhs=got_w[:].bitcast(U8).bitcast(FP4X4),
                rhs_scale=got_s[:],
                start=True,
                stop=True,
            )
            kn.append(fresh)
            dl.append(sb.tile([P, I], F32, name=f"dl{t}", tag=f"weighed{t}", align_bytes=64))

        def gather(t):
            old.append(sb.tile([P, I], F32, name=f"old{t}", tag="old" if t >= 1 else "old0", align_bytes=64))
            listed = key_planes[t][:].indirect(offsets[:])
            if t == 1:
                nc.scalar.activation(old[t][:], listed, ACT.Copy)
            else:
                nc.vector.tensor_copy(old[t][:], listed)

        def subtract(t):
            diff.append(sb.tile([P, I], F32, name=f"diff{t}", tag="diff" if t < 3 else "diff3", align_bytes=64))
            nc.vector.tensor_tensor(diff[t][:], kn[t], old[t][:], ALU.subtract)

        def weigh(t):
            nc.vector.tensor_tensor(
                dl[t][:].rearrange("p (n e) -> p n e", e=2),
                diff[t][:].rearrange("p (n e) -> p n e", e=2),
                trust_all.rearrange("p e n -> p n e"),
                ALU.mult,
            )

        def scatter(t):
            nc.scalar.activation(df[t][:].indirect(offsets[:]), dl[t][:], ACT.Copy)

        gather(0)
        gather(1)
        subtract(0)
        weigh(0)
        subtract(1)
        weigh(1)
        gather(2)
        subtract(2)
        weigh(2)
        gather(3)
        subtract(3)
        weigh(3)
        for t in range(PACK):
            scatter(t)

        km_planes = [
            sb.tile([P, PACK, BANK], BF16, name=f"km_planes{h}", tag=("diff", "old")[h], align_bytes=64) for h in range(HALVES)
        ]
        q_bf = sb.tile([P, Q * PACK], BF16, name="q_bf", tag="weighed3", align_bytes=64)
        q_codes = sb.tile([P, Q], U32, name="q_codes", align_bytes=64)
        q_scales = sb.tile([P, Q], U8, name="q_scales", align_bytes=64)

        def repair(t):
            for h in range(HALVES):
                cols = slice(h * BANK, (h + 1) * BANK)
                nc.vector.tensor_tensor(km_planes[h][:, t, :], df[t][:, cols], key_planes[t][:, cols], ALU.add)

        for t in range(PACK - 1):
            repair(t)
        for half in range(2):
            deal(nc.scalar.copy, q_bf, q_raw[half], half, slice(0, PACK))
        repair(PACK - 1)

        km_codes = sb.tile([P, T], U32, name="km_codes", align_bytes=64)
        km_scales = sb.tile([P, T], U8, name="km_scales", align_bytes=64)
        km_bf = [sb.tile([P, BANK * PACK], BF16, name=f"km_bf{h}", align_bytes=64) for h in range(HALVES)]
        weave(nc.vector.tensor_copy, km_bf[0], km_planes[0][:])
        weave(nc.scalar.copy, km_bf[1], km_planes[1][:])
        quantize(nc, q_codes, q_scales, slice(0, Q), q_bf)
        quantize(nc, km_codes, km_scales, slice(0, BANK), km_bf[0])

        neg_half = sb.tile([P, PACK, HALVES], F32, name="neg_half")
        neg_max = sb.tile([P, PACK], F32, name="neg_max")
        sum_half = sb.tile([P, PACK, HALVES], F32, name="sum_half")
        rescale = sb.tile([P, PACK, HALVES], F32, name="rescale")
        share = sb.tile([P, PACK, HALVES], F32, name="share")
        total = sb.tile([P, PACK], F32, name="total")
        inverse = sb.tile([P, PACK], F32, name="inverse")
        y = sb.tile([P, PACK, T], F32, name="y")
        y_rows = out_0.rearrange("(p r) c -> p r c", r=PACK)
        weights = [sb.tile([P, T], F32, name=f"p{r}") for r in range(PACK)]

        def score(r, h):
            rows = slice(r * P, (r + 1) * P)
            cols = slice(h * BANK, (h + 1) * BANK)
            bank = ps.tile([P, BANK], F32, name=f"a{r}{h}", tag=f"bank{2 * r + h}")
            nc.tensor.matmul_mx(
                out=bank[:],
                lhsT=q_codes[:, rows].bitcast(FP8X4),
                lhsT_scale=q_scales[:, rows],
                rhs=km_codes[:, cols].bitcast(FP8X4),
                rhs_scale=km_scales[:, cols],
                start=True,
                stop=True,
            )
            nc.vector.tensor_reduce(neg_half[:, r, h : h + 1], bank[:], AXIS.X, ALU.max, negate=True)
            nc.scalar.activation(
                weights[r][:, cols], bank[:], ACT.Exp, bias=neg_half[:, r, h : h + 1], accum_out=sum_half[:, r, h : h + 1]
            )

        def join(r):
            one = slice(r, r + 1)
            nc.vector.tensor_tensor(neg_max[:, one], neg_half[:, r, 0:1], neg_half[:, r, 1:2], ALU.min)
            nc.scalar.activation(rescale[:, r, :], neg_half[:, r, :], ACT.Exp, bias=neg_max[:, one], scale=-1.0)

        def invert(r):
            one = slice(r, r + 1)
            nc.vector.scalar_tensor_tensor(
                share[:, r, :], sum_half[:, r, :], 1.0 / 512.0, rescale[:, r, :], ALU.mult, ALU.mult, accum_out=total[:, one]
            )
            nc.vector.reciprocal(inverse[:, one], total[:, one])

        def normalise(r, h):
            cols = slice(h * BANK, (h + 1) * BANK)
            nc.vector.tensor_scalar(
                y[:, r, cols], weights[r][:, cols], rescale[:, r, h : h + 1], inverse[:, r : r + 1], ALU.mult, ALU.mult
            )

        def finish(r):
            normalise(r, 0)
            normalise(r, 1)
            nc.sync.dma_start(y_rows[:, r, :], y[:, r, :])

        score(0, 0)
        quantize(nc, km_codes, km_scales, slice(BANK, T), km_bf[1])
        score(1, 0)
        score(0, 1)
        join(0)
        score(1, 1)
        join(1)
        score(2, 0)
        invert(0)
        score(2, 1)
        join(2)
        finish(0)
        invert(1)
        score(3, 0)
        score(3, 1)
        join(3)
        finish(1)
        invert(2)
        finish(2)
        invert(3)
        normalise(3, 1)
        normalise(3, 0)
        nc.sync.dma_start(y_rows[:, 3, :], y[:, 3, :])

        y_codes = sb.tile([P, T], U32, name="y_codes", align_bytes=64)
        y_scales = sb.tile([P, T], U8, name="y_scales", align_bytes=64)
        word_rows = out_1[0].rearrange("p c t -> p (c t)").bitcast(I32)
        units = (slice(0, 256), slice(256, 640), slice(640, T))
        y_bf = [sb.tile([P, (c.stop - c.start) * PACK], BF16, name=f"y_bf{u}", align_bytes=64) for u, c in enumerate(units)]
        weave(nc.scalar.copy, y_bf[2], y[:, :, units[2]])
        weave(nc.vector.tensor_copy, y_bf[0], y[:, :, units[0]])
        weave(nc.vector.tensor_copy, y_bf[1], y[:, :, units[1]])
        for u, cols in enumerate(units):
            quantize(nc, y_codes, y_scales, cols, y_bf[u])
            nc.sync.dma_start(word_rows[:, cols], y_codes[:, cols].bitcast(I32))
        for quad in range(4):
            queue = nc.scalar if quad % 2 else nc.sync
            queue.dma_start(
                out_2[0, 4 * quad : 4 * quad + 4, :].bitcast(I32), y_scales[32 * quad : 32 * quad + 4, :].bitcast(I32)
            )
